import numpy as np
import ml_dtypes


def mxq(x, axis, fmt="e4m3"):
    dtype, down = {"e4m3": (ml_dtypes.float8_e4m3fn, 7), "e5m2": (ml_dtypes.float8_e5m2, 14)}[fmt]
    v = np.moveaxis(np.asarray(x, np.float32).astype(ml_dtypes.bfloat16).astype(np.float64), axis, -1)
    blocks = v.reshape(v.shape[:-1] + (-1, 32))
    amax = np.abs(blocks).max(-1, keepdims=True)
    byte = np.maximum(np.where(amax > 0, np.frexp(amax)[1] - 1 + 127, 0) - down, 1)
    scale = np.exp2(byte - 127.0)
    codes = (blocks / scale).astype(np.float32).astype(dtype).astype(np.float64)
    return np.moveaxis((codes * scale).reshape(v.shape), -1, axis)


WIDE = False


def mx_kscale(k):
    if not WIDE:
        return np.ones(k)
    levels = np.array([10, -10, 5, -5, 0])
    if k % 512:
        return np.exp2(np.random.permutation(np.resize(levels, k // 32))).repeat(32)
    a = np.empty((k // 512, 16))
    for p in range(k // 512):
        a[p, :8] = np.random.permutation(np.resize(levels, 8))
        for g in range(8):
            far = levels[np.abs(levels - a[p, g]) >= 10]
            a[p, g + 8] = far[np.random.randint(len(far))]
    return np.exp2(a.ravel()).repeat(32)


BF16 = ml_dtypes.bfloat16


def bf(x):
    return np.asarray(x, np.float32).astype(BF16)


def f64(x):
    return np.asarray(x).astype(np.float64)


B, S, D, M, N, C = 2, 1024, 512, 512, 512, 2


def cauchy_parts(om, nu, b):
    de = om[:, None] - nu[None, :]
    w = b[None, :] / (0.25 + de * de)
    gr = 0.5 * w
    gi = -de * w
    return gr, gi


def draw0():
    s, t, r = mx_kscale(S), mx_kscale(M), mx_kscale(N)
    return {"x": bf(np.random.standard_normal((B, S, D)) / s[None, :, None]),
            "p": bf(np.random.standard_normal((M, S)) / np.sqrt(S) * s[None, :] * t[:, None]),
            "om": bf(np.random.uniform(-4.0, 4.0, M)),
            "nu": bf(np.random.uniform(-4.0, 4.0, N)),
            "b": bf(np.random.standard_normal(N) * r),
            "c": bf(np.random.standard_normal((N, D)) * 1.5 / np.sqrt(N) / r[:, None]),
            "q": bf(np.random.standard_normal((C, S, M)) / np.sqrt(M) / t[None, None, :])}


def core(x, p, om, nu, b, c, q):
    gr, gi = cauchy_parts(f64(om), f64(nu), f64(b))
    gr, gi = gr, gi
    cq = mxq(f64(c), 0, "e4m3")
    kr = mxq(gr, 1, "e4m3") @ cq
    ki = mxq(gi, 1, "e4m3") @ cq
    u = mxq(f64(p), 1, "e4m3") @ mxq(f64(x), 1, "e4m3")
    fr = kr[None, :, :] * u
    fi = ki[None, :, :] * u
    qq = mxq(f64(q), 2, "e4m3")
    return (qq[0] @ mxq(fr, 1, "e4m3")) - (qq[1] @ mxq(fi, 1, "e4m3"))


def e4m3fn_bytes(y):
    return np.clip(np.asarray(y, np.float64), -448.0, 448.0).astype(np.float32).astype(ml_dtypes.float8_e4m3fn).view(np.uint8)


def e4m3fn_values(b):
    return np.asarray(b, np.uint8).view(ml_dtypes.float8_e4m3fn).astype(np.float64)


def setup_inputs():
    d = draw0()
    x0 = np.asarray(d['x']).astype(np.float64)
    s = (np.max(np.abs(x0), axis=(0, 2), keepdims=True) / 448.0).astype(np.float32)
    out = {}
    for k, v in d.items():
        if k == 'x':
            out['x_bytes'] = e4m3fn_bytes(x0 / s.astype(np.float64))
            out['x_scale'] = s
        else:
            out[k] = v
    return out


def reference(x_bytes, x_scale, p, om, nu, b, c, q):
    return core(e4m3fn_values(x_bytes) * x_scale.astype(np.float64), p, om, nu, b, c, q)

@@ -1,0 +1,314 @@
+from contextlib import ExitStack
+
+import concourse.mybir as mybir
+from concourse.masks import make_identity
+
+F32 = mybir.dt.float32
+BF16 = mybir.dt.bfloat16
+U32 = mybir.dt.uint32
+U8 = mybir.dt.uint8
+FP8 = mybir.dt.float8_e4m3fn
+FP8X4 = mybir.dt.float8_e4m3fn_x4
+ACT = mybir.ActivationFunctionType
+ALU = mybir.AluOpType
+
+P = 128
+B, S, D, M, N, C = 2, 1024, 512, 512, 512, 2
+G = S // 512
+DC = D // P
+SB = S // P
+
+FLOPS = 2 * C * M * N * D + 2 * B * M * S * D + 2 * B * C * S * M * D
+
+
+def tile_cauchytransferfunctionfilter_kernel(tc, x_bytes, x_scale, p, om, nu, b, c, q, out):
+    nc = tc.nc
+    with ExitStack() as ctx:
+        sb = ctx.enter_context(tc.tile_pool(name="sb", bufs=1))
+        outp = ctx.enter_context(tc.tile_pool(name="outp", bufs=7))
+        ps_u = ctx.enter_context(tc.psum_pool(name="ps_u", bufs=2))
+        ps_w = ctx.enter_context(tc.psum_pool(name="ps_w", bufs=6))
+        ctx.enter_context(tc.manual_schedule())
+
+        om_row = sb.tile([P, M], BF16, name="om_row")
+        nu_row = sb.tile([P, N], BF16, name="nu_row")
+        ident = sb.tile([P, P], F32, name="ident")
+        b4 = sb.tile([P, 4], BF16, name="b4")
+        b2 = sb.tile([P, 4], F32, name="b2")
+        xs = sb.tile([P, G, 4], F32, name="xs")
+        scr = sb.tile([P, 2], F32, name="scr")
+        x_in = [sb.tile([P, G, 4, D], U8, name=f"x_in{i}") for i in range(B)]
+        c_in = sb.tile([P, 4, D], BF16, name="c_in")
+        p_in = [sb.tile([P, 4, 512], BF16, name=f"p_in{g}") for g in range(G)]
+        q_in = [sb.tile([P, SB, M], BF16, name=f"q_in{r}") for r in range(C)]
+        x_wide = [[sb.tile([P, 4, D], BF16, name=f"x_wide{i}{g}") for g in range(G)] for i in range(B)]
+
+        def mx(width, name):
+            codes = sb.tile([P, width], U32, name=name + "_codes", align_bytes=64)
+            scales = sb.tile([P, width], U8, name=name + "_scales", align_bytes=64)
+            grouped = sb.tile([P, width * 4], BF16, name=name + "_grp", align_bytes=64)
+            return codes, scales, grouped
+
+        gr_q = mx(M, "gr")
+        gi_q = mx(M, "gi")
+        c_q = mx(D, "c")
+        p_q = [mx(M, f"p{g}") for g in range(G)]
+        x_q = [[mx(D, f"x{i}{g}") for g in range(G)] for i in range(B)]
+        q_q = [mx(S, f"q{r}") for r in range(C)]
+        f_codes = [[sb.tile([P, D], U32, name=f"f_codes{i}{r}", align_bytes=64) for r in range(C)] for i in range(B)]
+        f_scales = [[sb.tile([P, D], U8, name=f"f_scales{i}{r}", align_bytes=64) for r in range(C)] for i in range(B)]
+        f_grp = [sb.tile([P, C, D * 4], BF16, name=f"f_grp{i}", align_bytes=64) for i in range(B)]
+        sq = sb.tile([P, M * 4], F32, name="sq")
+        rt = sb.tile([P, M * 4], F32, name="rt")
+        rr = sq
+        g32 = sb.tile([P, M * 4], F32, name="g32")
+        k_sb = sb.tile([P, DC, C, P * 4], F32, name="k_sb")
+
+        def quant(t, a, z):
+            codes, scales, grouped = t
+            nc.vector.quantize_mx(out=codes[:, a:z].bitcast(FP8X4), scales=scales[:, a:z], in_=grouped[:, 4 * a : 4 * z])
+
+        def mxmm(acc, lhs, m0, rhs, n0, n, start, stop):
+            nc.tensor.matmul_mx(
+                out=acc,
+                lhsT=lhs[0][:, m0 : m0 + P].bitcast(FP8X4),
+                lhsT_scale=lhs[1][:, m0 : m0 + P],
+                rhs=rhs[0][:, n0 : n0 + n].bitcast(FP8X4),
+                rhs_scale=rhs[1][:, n0 : n0 + n],
+                start=start,
+                stop=stop,
+            )
+
+        nc.sync.dma_start(out=om_row[127:128, :], in_=om.rearrange("(o m) -> o m", o=1))
+        nc.sync.dma_start(out=nu_row[63:64, :], in_=nu.rearrange("(o m) -> o m", o=1))
+        nc.vector.memset(scr[:], 1.0)
+        nc.gpsimd.memset(om_row[0:32, :], 0.0)
+        nc.vector.memset(om_row[32:64, :], -1.0)
+        nc.gpsimd.memset(om_row[64:127, :], 0.0)
+        nc.gpsimd.memset(nu_row[0:32, :], 0.0)
+        nc.gpsimd.memset(nu_row[32:63, :], 0.0)
+        nc.vector.memset(nu_row[64:128, :], 1.0)
+        make_identity(nc, ident[:])
+        nc.scalar.dma_start(out=xs[:], in_=x_scale.rearrange("o (g p t) q -> p g (o t q)", p=P, t=4))
+        nc.scalar.dma_start(out=b4[:], in_=b.rearrange("(p t) -> p t", t=4))
+        nc.sync.dma_start(out=x_in[0][:], in_=x_bytes[0].rearrange("(g p t) d -> p g t d", p=P, t=4))
+        nc.sync.dma_start(out=c_in[:], in_=c.rearrange("(p t) d -> p t d", t=4))
+        for g in range(G):
+            nc.sync.dma_start(out=p_in[g][:], in_=p.rearrange("(r t) s -> r t s", t=4)[:, :, 512 * g : 512 * (g + 1)])
+        nc.sync.dma_start(out=x_in[1][:], in_=x_bytes[1].rearrange("(g p t) d -> p g t d", p=P, t=4))
+        for r in range(C):
+            for h in range(2):
+                nc.sync.dma_start(
+                    out=q_in[r][:, 4 * h : 4 * h + 4, :],
+                    in_=q[r].rearrange("(j k) m -> j k m", k=SB)[:, 4 * h : 4 * h + 4, :],
+                )
+        nc.scalar.activation(scr[:, 1:2], scr[:, 0:1], ACT.Abs_reciprocal_sqrt)
+        e_ps = [ps_w.tile([P, P, 4], F32, name="w") for t in range(4)]
+        for k in range(4):
+            for t in range(4):
+                nc.tensor.matmul(e_ps[k][:, :, t], nu_row[:, t::4], om_row[:, k::4], start=True, stop=True)
+
+        def chunk(tile, t, n=1):
+            return tile[:, 512 * t : 512 * (t + n)]
+
+        def g_square(t):
+            nc.scalar.activation(chunk(sq, t), e_ps[t][:].rearrange("p m t -> p (m t)"), ACT.Square, scale=2.0)
+
+        def g_rsqrt(t):
+            nc.scalar.activation(chunk(rt, t, 2), chunk(sq, t, 2), ACT.Abs_reciprocal_sqrt, bias=1.0)
+
+        def g_recip(t):
+            nc.scalar.activation(chunk(rr, t, 2), chunk(rt, t, 2), ACT.Square)
+
+        def g_real(t):
+            nc.vector.tensor_tensor(
+                chunk(g32, t, 2).rearrange("p (m t) -> p m t", t=4),
+                chunk(rr, t, 2).rearrange("p (m t) -> p m t", t=4),
+                b2[:].unsqueeze(1).to_broadcast([P, 2 * P, 4]),
+                op=ALU.mult,
+            )
+
+        def g_imag(t):
+            nc.vector.scalar_tensor_tensor(
+                chunk(gi_q[2], t), e_ps[t][:].rearrange("p m t -> p (m t)"), 2.0, chunk(g32, t), op0=ALU.mult, op1=ALU.mult
+            )
+
+        def g_round(t, n):
+            nc.scalar.copy(chunk(gr_q[2], t, n), chunk(g32, t, n))
+
+        def widen_v(i, g, t):
+            nc.vector.tensor_scalar(x_wide[i][g][:, t, :], x_in[i][:, g, t, :].bitcast(FP8), xs[:, g, t : t + 1], None, op0=ALU.mult)
+
+        def widen_s(i, g, t):
+            nc.scalar.activation(x_wide[i][g][:, t, :], x_in[i][:, g, t, :].bitcast(FP8), ACT.Copy, scale=xs[:, g, t : t + 1])
+
+        def interleave(grouped, src):
+            nc.vector.tensor_copy(
+                grouped[:].rearrange("p (c i t) -> p c t i", i=4, t=4), src[:].rearrange("p t (c i) -> p c t i", i=4)
+            )
+
+        def p_turn(g, h):
+            bank = ps_w.tile([P, 2, 2, P], F32, name="w")
+            for k in range(2):
+                words = p_in[g][:, 2 * h + k, :].bitcast(F32)
+                for u in range(2):
+                    nc.tensor.transpose(bank[:, k, u, :], words[:, u::2], ident[:])
+            return bank
+
+        def q_turn(r, h):
+            bank = ps_w.tile([P, 2, 2, P], F32, name="w")
+            for k in range(2):
+                words = q_in[r][:, 2 * h + k, :].bitcast(F32)
+                for u in range(2):
+                    nc.tensor.transpose(bank[:, k, u, :], words[:, u::2], ident[:])
+            return bank
+
+        def turn_copy(grouped, h, bank):
+            dst = grouped[:, 1024 * h : 1024 * (h + 1)].bitcast(F32).rearrange("p (k r u) -> p k r u", k=2, u=2)
+            nc.scalar.copy(dst, bank[:].rearrange("p k u r -> p k r u"))
+
+        def k_mm(dc, r):
+            bank = ps_w.tile([P, 4, P], F32, name="w")
+            for t in range(4):
+                mxmm(bank[:, t, :], (gr_q, gi_q)[r], P * t, c_q, P * dc, P, True, True)
+            return bank
+
+        def k_copy(dc, r, bank):
+            nc.scalar.copy(
+                k_sb[:, dc, r, :].rearrange("p (d t) -> p d t", t=4), bank[:].rearrange("p t d -> p d t")
+            )
+
+        def u_mm(i, dc):
+            bank = ps_u.tile([P, 4, P], F32, name="u")
+            for t in range(4):
+                for g in range(G):
+                    mxmm(bank[:, t, :], p_q[g], P * t, x_q[i][g], P * dc, P, g == 0, g == G - 1)
+            return bank
+
+        def f_mul(i, dc, bank):
+            nc.vector.tensor_tensor(
+                f_grp[i][:, :, 512 * dc : 512 * (dc + 1)].rearrange("p r (d t) -> p r d t", t=4),
+                bank[:].rearrange("p t d -> p d t").unsqueeze(1).to_broadcast([P, C, P, 4]),
+                k_sb[:, dc, :, :].rearrange("p r (d t) -> p r d t", t=4),
+                op=ALU.mult,
+            )
+
+        def f_quant(i, h):
+            for r in range(C):
+                nc.vector.quantize_mx(
+                    out=f_codes[i][r][:, 256 * h : 256 * (h + 1)].bitcast(FP8X4),
+                    scales=f_scales[i][r][:, 256 * h : 256 * (h + 1)],
+                    in_=f_grp[i][:, r, 1024 * h : 1024 * (h + 1)],
+                )
+
+        def o_mm(i, h, s):
+            bank = ps_w.tile([P, 256], F32, name="w")
+            for r in range(C):
+                mxmm(bank[:], q_q[r], P * s, (f_codes[i][r], f_scales[i][r]), 256 * h, 256, r == 0, r == C - 1)
+            return bank
+
+        def out_quad(i, h, s4, vec=()):
+            o_sb = outp.tile([P, 4, 256], F32, name="o_sb")
+            for k in range(4):
+                bank = o_mm(i, h, 4 * s4 + k)
+                if k in vec:
+                    nc.vector.tensor_copy(o_sb[:, k, :], bank[:])
+                else:
+                    nc.scalar.copy(o_sb[:, k, :], bank[:])
+            nc.sync.dma_start(
+                out=out[i].rearrange("(j k) d -> j k d", k=SB)[:, 4 * s4 : 4 * s4 + 4, 256 * h : 256 * (h + 1)], in_=o_sb[:]
+            )
+
+        for g in range(G):
+            for t in range(4):
+                widen_v(0, g, t)
+        for t in range(4):
+            g_square(t)
+        for t in (0, 2):
+            g_rsqrt(t)
+        for t in (0, 2):
+            g_recip(t)
+        interleave(c_q[2], c_in)
+        quant(c_q, 0, D)
+        nc.vector.tensor_scalar(b2[:], b4[:], 2.0, None, op0=ALU.mult)
+        interleave(x_q[0][0][2], x_wide[0][0])
+        for h in range(2):
+            turn_copy(p_q[0][2], h, p_turn(0, h))
+        widen_s(1, 0, 0)
+        widen_s(1, 0, 1)
+        g_real(0)
+        g_real(2)
+        g_round(0, 2)
+        for t in range(4):
+            g_imag(t)
+        g_round(2, 2)
+        for h in range(2):
+            turn_copy(p_q[1][2], h, p_turn(1, h))
+        interleave(x_q[0][1][2], x_wide[0][1])
+        quant(gi_q, 0, M)
+        quant(gr_q, 0, M)
+        for g in range(G):
+            quant(x_q[0][g], 0, D)
+        for g in range(G):
+            quant(p_q[g], 0, M)
+        widen_s(1, 0, 2)
+        widen_s(1, 0, 3)
+        k_bank = {}
+        u_bank = {}
+        interleave(x_q[1][0][2], x_wide[1][0])
+
+        def k_pair(h):
+            for r in (1, 0):
+                for dc in (2 * h, 2 * h + 1):
+                    k_bank[dc, r] = k_mm(dc, r)
+
+        def k_out(h):
+            for dc in (2 * h, 2 * h + 1):
+                for r in (1, 0):
+                    k_copy(dc, r, k_bank[dc, r])
+
+        k_pair(0)
+        k_out(0)
+        k_pair(1)
+        widen_s(1, 1, 0)
+        widen_s(1, 1, 1)
+        for dc in range(2):
+            u_bank[dc] = u_mm(0, dc)
+        k_out(1)
+        for dc in range(2):
+            f_mul(0, dc, u_bank[dc])
+        u_bank[2] = u_mm(0, 2)
+        f_mul(0, 2, u_bank[2])
+        f_quant(0, 0)
+        u_bank[3] = u_mm(0, 3)
+        f_mul(0, 3, u_bank[3])
+        widen_s(1, 1, 2)
+        widen_s(1, 1, 3)
+        interleave(x_q[1][1][2], x_wide[1][1])
+        f_quant(0, 1)
+        for half in range(2):
+            for r in range(C):
+                for h in (2 * half, 2 * half + 1):
+                    turn_copy(q_q[r][2], h, q_turn(r, h))
+            for r in range(C):
+                quant(q_q[r], 512 * half, 512 * (half + 1))
+            if half == 0:
+                for g in range(G):
+                    quant(x_q[1][g], 0, D)
+        out_quad(0, 0, 0)
+        for dc in range(2):
+            u_bank[dc] = u_mm(1, dc)
+            f_mul(1, dc, u_bank[dc])
+        out_quad(0, 0, 1)
+        u_bank[2] = u_mm(1, 2)
+        f_mul(1, 2, u_bank[2])
+        f_quant(1, 0)
+        out_quad(0, 1, 0)
+        u_bank[3] = u_mm(1, 3)
+        f_mul(1, 3, u_bank[3])
+        f_quant(1, 1)
+        out_quad(0, 1, 1)
+        out_quad(1, 0, 0)
+        out_quad(1, 0, 1, (1, 3))
+        out_quad(1, 1, 0, (0, 2))
+        out_quad(1, 1, 1, (0, 2))

@@ -25,7 +25,7 @@ def tile_cauchytransferfunctionfilter_kernel(tc, x_bytes, x_scale, p, om, nu, b,
     nc = tc.nc
     with ExitStack() as ctx:
         sb = ctx.enter_context(tc.tile_pool(name="sb", bufs=1))
-        outp = ctx.enter_context(tc.tile_pool(name="outp", bufs=7))
+        outp = ctx.enter_context(tc.tile_pool(name="outp", bufs=12))
         ps_u = ctx.enter_context(tc.psum_pool(name="ps_u", bufs=2))
         ps_w = ctx.enter_context(tc.psum_pool(name="ps_w", bufs=6))
         ctx.enter_context(tc.manual_schedule())
@@ -36,6 +36,7 @@ def tile_cauchytransferfunctionfilter_kernel(tc, x_bytes, x_scale, p, om, nu, b,
         b4 = sb.tile([P, 4], BF16, name="b4")
         b2 = sb.tile([P, 4], F32, name="b2")
         xs = sb.tile([P, G, 4], F32, name="xs")
+        warm = sb.tile([P, D], BF16, name="warm")
         scr = sb.tile([P, 2], F32, name="scr")
         x_in = [sb.tile([P, G, 4, D], U8, name=f"x_in{i}") for i in range(B)]
         c_in = sb.tile([P, 4, D], BF16, name="c_in")
@@ -81,6 +82,7 @@ def tile_cauchytransferfunctionfilter_kernel(tc, x_bytes, x_scale, p, om, nu, b,
 
         nc.sync.dma_start(out=om_row[127:128, :], in_=om.rearrange("(o m) -> o m", o=1))
         nc.sync.dma_start(out=nu_row[63:64, :], in_=nu.rearrange("(o m) -> o m", o=1))
+        nc.vector.memset(warm[:], 0.0)
         nc.vector.memset(scr[:], 1.0)
         nc.gpsimd.memset(om_row[0:32, :], 0.0)
         nc.vector.memset(om_row[32:64, :], -1.0)
@@ -91,19 +93,28 @@ def tile_cauchytransferfunctionfilter_kernel(tc, x_bytes, x_scale, p, om, nu, b,
         make_identity(nc, ident[:])
         nc.scalar.dma_start(out=xs[:], in_=x_scale.rearrange("o (g p t) q -> p g (o t q)", p=P, t=4))
         nc.scalar.dma_start(out=b4[:], in_=b.rearrange("(p t) -> p t", t=4))
-        nc.sync.dma_start(out=x_in[0][:], in_=x_bytes[0].rearrange("(g p t) d -> p g t d", p=P, t=4))
+        for g in range(G):
+            nc.sync.dma_start(out=x_in[0][:, g], in_=x_bytes[0].rearrange("(g p t) d -> p g t d", p=P, t=4)[:, g])
         nc.sync.dma_start(out=c_in[:], in_=c.rearrange("(p t) d -> p t d", t=4))
         for g in range(G):
             nc.sync.dma_start(out=p_in[g][:], in_=p.rearrange("(r t) s -> r t s", t=4)[:, :, 512 * g : 512 * (g + 1)])
+        q_load = lambda r, h: nc.sync.dma_start(
+            out=q_in[r][:, 4 * h : 4 * h + 4, :],
+            in_=q[r].rearrange("(j k) m -> j k m", k=SB)[:, 4 * h : 4 * h + 4, :],
+        )
+        q_load(0, 0)
+        q_load(1, 0)
         nc.sync.dma_start(out=x_in[1][:], in_=x_bytes[1].rearrange("(g p t) d -> p g t d", p=P, t=4))
-        for r in range(C):
-            for h in range(2):
-                nc.sync.dma_start(
-                    out=q_in[r][:, 4 * h : 4 * h + 4, :],
-                    in_=q[r].rearrange("(j k) m -> j k m", k=SB)[:, 4 * h : 4 * h + 4, :],
-                )
+        q_load(0, 1)
+        q_load(1, 1)
         nc.scalar.activation(scr[:, 1:2], scr[:, 0:1], ACT.Abs_reciprocal_sqrt)
         e_ps = [ps_w.tile([P, P, 4], F32, name="w") for t in range(4)]
+        def keep_warm(bank):
+            flat = bank[:].rearrange("p a b -> p (a b)") if len(bank.shape) == 3 else bank[:]
+            nc.tensor.matmul(flat, warm[:, 0:P], warm[:], start=True, stop=True)
+
+        for k in range(4):
+            keep_warm(e_ps[0])
         for k in range(4):
             for t in range(4):
                 nc.tensor.matmul(e_ps[k][:, :, t], nu_row[:, t::4], om_row[:, k::4], start=True, stop=True)
@@ -134,7 +145,7 @@ def tile_cauchytransferfunctionfilter_kernel(tc, x_bytes, x_scale, p, om, nu, b,
             )
 
         def g_round(t, n):
-            nc.scalar.copy(chunk(gr_q[2], t, n), chunk(g32, t, n))
+            nc.gpsimd.tensor_scalar(chunk(gr_q[2], t, n), chunk(g32, t, n), 1.0, 0.0, op0=ALU.mult, op1=ALU.add)
 
         def widen_v(i, g, t):
             nc.vector.tensor_scalar(x_wide[i][g][:, t, :], x_in[i][:, g, t, :].bitcast(FP8), xs[:, g, t : t + 1], None, op0=ALU.mult)
@@ -148,7 +159,7 @@ def tile_cauchytransferfunctionfilter_kernel(tc, x_bytes, x_scale, p, om, nu, b,
             )
 
         def p_turn(g, h):
-            bank = ps_w.tile([P, 2, 2, P], F32, name="w")
+            bank = ps_u.tile([P, 2, 2, P], F32, name="u")
             for k in range(2):
                 words = p_in[g][:, 2 * h + k, :].bitcast(F32)
                 for u in range(2):
@@ -167,8 +178,10 @@ def tile_cauchytransferfunctionfilter_kernel(tc, x_bytes, x_scale, p, om, nu, b,
             dst = grouped[:, 1024 * h : 1024 * (h + 1)].bitcast(F32).rearrange("p (k r u) -> p k r u", k=2, u=2)
             nc.scalar.copy(dst, bank[:].rearrange("p k u r -> p k r u"))
 
-        def k_mm(dc, r):
+        def k_mm(dc, r, warm_first=False):
             bank = ps_w.tile([P, 4, P], F32, name="w")
+            if warm_first:
+                keep_warm(bank)
             for t in range(4):
                 mxmm(bank[:, t, :], (gr_q, gi_q)[r], P * t, c_q, P * dc, P, True, True)
             return bank
@@ -178,8 +191,10 @@ def tile_cauchytransferfunctionfilter_kernel(tc, x_bytes, x_scale, p, om, nu, b,
                 k_sb[:, dc, r, :].rearrange("p (d t) -> p d t", t=4), bank[:].rearrange("p t d -> p d t")
             )
 
-        def u_mm(i, dc):
+        def u_mm(i, dc, warm_first=False):
             bank = ps_u.tile([P, 4, P], F32, name="u")
+            if warm_first:
+                keep_warm(bank)
             for t in range(4):
                 for g in range(G):
                     mxmm(bank[:, t, :], p_q[g], P * t, x_q[i][g], P * dc, P, g == 0, g == G - 1)
@@ -201,114 +216,142 @@ def tile_cauchytransferfunctionfilter_kernel(tc, x_bytes, x_scale, p, om, nu, b,
                     in_=f_grp[i][:, r, 1024 * h : 1024 * (h + 1)],
                 )
 
-        def o_mm(i, h, s):
-            bank = ps_w.tile([P, 256], F32, name="w")
-            for r in range(C):
-                mxmm(bank[:], q_q[r], P * s, (f_codes[i][r], f_scales[i][r]), 256 * h, 256, r == 0, r == C - 1)
+        def o_mm(i, h, s2, warm_first=False):
+            bank = ps_w.tile([P, 2, 256], F32, name="w")
+            if warm_first:
+                keep_warm(bank)
+            for k in range(2):
+                for r in range(C):
+                    mxmm(bank[:, k, :], q_q[r], P * (2 * s2 + k), (f_codes[i][r], f_scales[i][r]), 256 * h, 256, r == 0, r == C - 1)
             return bank
 
-        def out_quad(i, h, s4, vec=()):
-            o_sb = outp.tile([P, 4, 256], F32, name="o_sb")
-            for k in range(4):
-                bank = o_mm(i, h, 4 * s4 + k)
-                if k in vec:
-                    nc.vector.tensor_copy(o_sb[:, k, :], bank[:])
-                else:
-                    nc.scalar.copy(o_sb[:, k, :], bank[:])
+        def out_pair(i, h, s2, on_vector=False, warm_first=False):
+            bank = o_mm(i, h, s2, warm_first)
+            o_sb = outp.tile([P, 2, 256], F32, name="o_sb")
+            if on_vector:
+                nc.vector.tensor_copy(o_sb[:], bank[:])
+            else:
+                nc.scalar.copy(o_sb[:], bank[:])
             nc.sync.dma_start(
-                out=out[i].rearrange("(j k) d -> j k d", k=SB)[:, 4 * s4 : 4 * s4 + 4, 256 * h : 256 * (h + 1)], in_=o_sb[:]
+                out=out[i].rearrange("(j k) d -> j k d", k=SB)[:, 2 * s2 : 2 * s2 + 2, 256 * h : 256 * (h + 1)], in_=o_sb[:]
             )
 
-        for g in range(G):
-            for t in range(4):
-                widen_v(0, g, t)
+        kb = {}
+        ub = {}
+        tq = {}
         for t in range(4):
-            g_square(t)
-        for t in (0, 2):
-            g_rsqrt(t)
-        for t in (0, 2):
-            g_recip(t)
+            widen_v(0, 0, t)
+        g_square(0)
+        g_square(1)
+        g_square(2)
+        g_rsqrt(0)
+        g_square(3)
+        g_recip(0)
+        g_rsqrt(2)
+        g_recip(2)
+        interleave(x_q[0][0][2], x_wide[0][0])
         interleave(c_q[2], c_in)
+        widen_v(0, 1, 0)
+        quant(x_q[0][0], 0, D)
+        widen_v(0, 1, 1)
         quant(c_q, 0, D)
         nc.vector.tensor_scalar(b2[:], b4[:], 2.0, None, op0=ALU.mult)
-        interleave(x_q[0][0][2], x_wide[0][0])
+        tp = [p_turn(0, 0), p_turn(0, 1)]
+        for r in range(C):
+            for h in range(2):
+                tq[r, h] = q_turn(r, h)
+        widen_s(0, 1, 2)
+        widen_s(0, 1, 3)
         for h in range(2):
-            turn_copy(p_q[0][2], h, p_turn(0, h))
-        widen_s(1, 0, 0)
-        widen_s(1, 0, 1)
+            turn_copy(p_q[0][2], h, tp[h])
         g_real(0)
-        g_real(2)
+        g_imag(0)
+        g_imag(1)
         g_round(0, 2)
-        for t in range(4):
-            g_imag(t)
+        g_real(2)
+        g_imag(2)
+        g_imag(3)
         g_round(2, 2)
+        tp = [p_turn(1, 0), p_turn(1, 1)]
+        widen_s(1, 0, 0)
+        turn_copy(q_q[0][2], 0, tq[0, 0])
+        turn_copy(q_q[0][2], 1, tq[0, 1])
+        widen_s(1, 0, 1)
+        turn_copy(q_q[1][2], 0, tq[1, 0])
+        turn_copy(q_q[1][2], 1, tq[1, 1])
         for h in range(2):
-            turn_copy(p_q[1][2], h, p_turn(1, h))
-        interleave(x_q[0][1][2], x_wide[0][1])
-        quant(gi_q, 0, M)
-        quant(gr_q, 0, M)
-        for g in range(G):
-            quant(x_q[0][g], 0, D)
-        for g in range(G):
-            quant(p_q[g], 0, M)
+            turn_copy(p_q[1][2], h, tp[h])
         widen_s(1, 0, 2)
+        quant(p_q[0], 0, M)
+        quant(gr_q, 0, M)
+        quant(gi_q, 0, M)
+        interleave(x_q[0][1][2], x_wide[0][1])
+        quant(q_q[0], 0, 512)
+        quant(x_q[0][1], 0, D)
+        quant(q_q[1], 0, 512)
+        quant(p_q[1], 0, M)
+        for dc in range(2):
+            for r in range(C):
+                kb[dc, r] = k_mm(dc, r)
+        k_copy(0, 0, kb[0, 0])
         widen_s(1, 0, 3)
-        k_bank = {}
-        u_bank = {}
+        k_copy(0, 1, kb[0, 1])
         interleave(x_q[1][0][2], x_wide[1][0])
-
-        def k_pair(h):
-            for r in (1, 0):
-                for dc in (2 * h, 2 * h + 1):
-                    k_bank[dc, r] = k_mm(dc, r)
-
-        def k_out(h):
-            for dc in (2 * h, 2 * h + 1):
-                for r in (1, 0):
-                    k_copy(dc, r, k_bank[dc, r])
-
-        k_pair(0)
-        k_out(0)
-        k_pair(1)
+        ub[0] = u_mm(0, 0, True)
+        kb[2, 0] = k_mm(2, 0)
+        kb[2, 1] = k_mm(2, 1)
+        ub[1] = u_mm(0, 1)
+        kb[3, 0] = k_mm(3, 0)
+        kb[3, 1] = k_mm(3, 1)
+        k_copy(1, 0, kb[1, 0])
+        k_copy(1, 1, kb[1, 1])
+        k_copy(2, 0, kb[2, 0])
+        k_copy(2, 1, kb[2, 1])
         widen_s(1, 1, 0)
-        widen_s(1, 1, 1)
-        for dc in range(2):
-            u_bank[dc] = u_mm(0, dc)
-        k_out(1)
-        for dc in range(2):
-            f_mul(0, dc, u_bank[dc])
-        u_bank[2] = u_mm(0, 2)
-        f_mul(0, 2, u_bank[2])
+        k_copy(3, 0, kb[3, 0])
+        k_copy(3, 1, kb[3, 1])
+        for t in range(1, 4):
+            widen_s(1, 1, t)
+        f_mul(0, 0, ub[0])
+        ub[2] = u_mm(0, 2)
+        f_mul(0, 1, ub[1])
+        ub[3] = u_mm(0, 3)
+        f_mul(0, 2, ub[2])
         f_quant(0, 0)
-        u_bank[3] = u_mm(0, 3)
-        f_mul(0, 3, u_bank[3])
-        widen_s(1, 1, 2)
-        widen_s(1, 1, 3)
-        interleave(x_q[1][1][2], x_wide[1][1])
+        f_mul(0, 3, ub[3])
         f_quant(0, 1)
-        for half in range(2):
-            for r in range(C):
-                for h in (2 * half, 2 * half + 1):
-                    turn_copy(q_q[r][2], h, q_turn(r, h))
-            for r in range(C):
-                quant(q_q[r], 512 * half, 512 * (half + 1))
-            if half == 0:
-                for g in range(G):
-                    quant(x_q[1][g], 0, D)
-        out_quad(0, 0, 0)
-        for dc in range(2):
-            u_bank[dc] = u_mm(1, dc)
-            f_mul(1, dc, u_bank[dc])
-        out_quad(0, 0, 1)
-        u_bank[2] = u_mm(1, 2)
-        f_mul(1, 2, u_bank[2])
+        for r in range(C):
+            tq[r, 2] = q_turn(r, 2)
+        for r in range(C):
+            turn_copy(q_q[r][2], 2, tq[r, 2])
+        out_pair(0, 0, 0, False, True)
+        for r in range(C):
+            tq[r, 3] = q_turn(r, 3)
+        turn_copy(q_q[0][2], 3, tq[0, 3])
+        out_pair(0, 0, 1)
+        turn_copy(q_q[1][2], 3, tq[1, 3])
+        out_pair(0, 1, 0)
+        out_pair(0, 1, 1)
+        interleave(x_q[1][1][2], x_wide[1][1])
+        quant(x_q[1][0], 0, D)
+        quant(x_q[1][1], 0, D)
+        quant(q_q[0], 512, 1024)
+        quant(q_q[1], 512, 1024)
+        ub[0] = u_mm(1, 0)
+        ub[1] = u_mm(1, 1)
+        f_mul(1, 0, ub[0])
+        f_mul(1, 1, ub[1])
+        out_pair(0, 0, 2)
+        out_pair(0, 0, 3)
+        ub[2] = u_mm(1, 2)
+        f_mul(1, 2, ub[2])
         f_quant(1, 0)
-        out_quad(0, 1, 0)
-        u_bank[3] = u_mm(1, 3)
-        f_mul(1, 3, u_bank[3])
+        out_pair(0, 1, 2)
+        ub[3] = u_mm(1, 3)
+        f_mul(1, 3, ub[3])
         f_quant(1, 1)
-        out_quad(0, 1, 1)
-        out_quad(1, 0, 0)
-        out_quad(1, 0, 1, (1, 3))
-        out_quad(1, 1, 0, (0, 2))
-        out_quad(1, 1, 1, (0, 2))
+        out_pair(0, 1, 3)
+        for s2 in range(4):
+            out_pair(1, 0, s2)
+        for s2 in range(4):
+            out_pair(1, 1, s2, s2 % 2 == 1)

@@ -25,7 +25,7 @@ def tile_cauchytransferfunctionfilter_kernel(tc, x_bytes, x_scale, p, om, nu, b,
     nc = tc.nc
     with ExitStack() as ctx:
         sb = ctx.enter_context(tc.tile_pool(name="sb", bufs=1))
-        outp = ctx.enter_context(tc.tile_pool(name="outp", bufs=12))
+        outp = ctx.enter_context(tc.tile_pool(name="outp", bufs=8))
         ps_u = ctx.enter_context(tc.psum_pool(name="ps_u", bufs=2))
         ps_w = ctx.enter_context(tc.psum_pool(name="ps_w", bufs=6))
         ctx.enter_context(tc.manual_schedule())
@@ -40,7 +40,7 @@ def tile_cauchytransferfunctionfilter_kernel(tc, x_bytes, x_scale, p, om, nu, b,
         scr = sb.tile([P, 2], F32, name="scr")
         x_in = [sb.tile([P, G, 4, D], U8, name=f"x_in{i}") for i in range(B)]
         c_in = sb.tile([P, 4, D], BF16, name="c_in")
-        p_in = [sb.tile([P, 4, 512], BF16, name=f"p_in{g}") for g in range(G)]
+        p_in = [sb.tile([P, 2, S], BF16, name=f"p_in{h}") for h in range(2)]
         q_in = [sb.tile([P, SB, M], BF16, name=f"q_in{r}") for r in range(C)]
         x_wide = [[sb.tile([P, 4, D], BF16, name=f"x_wide{i}{g}") for g in range(G)] for i in range(B)]
 
@@ -56,9 +56,11 @@ def tile_cauchytransferfunctionfilter_kernel(tc, x_bytes, x_scale, p, om, nu, b,
         p_q = [mx(M, f"p{g}") for g in range(G)]
         x_q = [[mx(D, f"x{i}{g}") for g in range(G)] for i in range(B)]
         q_q = [mx(S, f"q{r}") for r in range(C)]
-        f_codes = [[sb.tile([P, D], U32, name=f"f_codes{i}{r}", align_bytes=64) for r in range(C)] for i in range(B)]
-        f_scales = [[sb.tile([P, D], U8, name=f"f_scales{i}{r}", align_bytes=64) for r in range(C)] for i in range(B)]
-        f_grp = [sb.tile([P, C, D * 4], BF16, name=f"f_grp{i}", align_bytes=64) for i in range(B)]
+        units = [(0, 0, 256), (0, 256, 256), (1, 0, 256), (1, 256, 128), (1, 384, 128)]
+        f_codes = [sb.tile([P, C * w], U32, name=f"f_codes{n}", align_bytes=64) for n, (i, d0, w) in enumerate(units)]
+        f_scales = [sb.tile([P, C * w], U8, name=f"f_scales{n}", align_bytes=64) for n, (i, d0, w) in enumerate(units)]
+        f_grp = [sb.tile([P, C * w * 4], BF16, name=f"f_grp{n}", align_bytes=64) for n, (i, d0, w) in enumerate(units)]
+        o_all = [sb.tile([P, 2, D], F32, name=f"o_all{n}") for n in range(SB // 2)]
         sq = sb.tile([P, M * 4], F32, name="sq")
         rt = sb.tile([P, M * 4], F32, name="rt")
         rr = sq
@@ -96,8 +98,8 @@ def tile_cauchytransferfunctionfilter_kernel(tc, x_bytes, x_scale, p, om, nu, b,
         for g in range(G):
             nc.sync.dma_start(out=x_in[0][:, g], in_=x_bytes[0].rearrange("(g p t) d -> p g t d", p=P, t=4)[:, g])
         nc.sync.dma_start(out=c_in[:], in_=c.rearrange("(p t) d -> p t d", t=4))
-        for g in range(G):
-            nc.sync.dma_start(out=p_in[g][:], in_=p.rearrange("(r t) s -> r t s", t=4)[:, :, 512 * g : 512 * (g + 1)])
+        for h in range(2):
+            nc.sync.dma_start(out=p_in[h][:], in_=p.rearrange("(r t) s -> r t s", t=4)[:, 2 * h : 2 * h + 2, :])
         q_load = lambda r, h: nc.sync.dma_start(
             out=q_in[r][:, 4 * h : 4 * h + 4, :],
             in_=q[r].rearrange("(j k) m -> j k m", k=SB)[:, 4 * h : 4 * h + 4, :],
@@ -110,7 +112,7 @@ def tile_cauchytransferfunctionfilter_kernel(tc, x_bytes, x_scale, p, om, nu, b,
         nc.scalar.activation(scr[:, 1:2], scr[:, 0:1], ACT.Abs_reciprocal_sqrt)
         e_ps = [ps_w.tile([P, P, 4], F32, name="w") for t in range(4)]
         def keep_warm(bank):
-            flat = bank[:].rearrange("p a b -> p (a b)") if len(bank.shape) == 3 else bank[:]
+            flat = bank[:].rearrange("p a b -> p (a b)") if len(bank.shape) == 3 else bank[:].rearrange("p a b c -> p (a b c)")
             nc.tensor.matmul(flat, warm[:, 0:P], warm[:], start=True, stop=True)
 
         for k in range(4):
@@ -158,16 +160,29 @@ def tile_cauchytransferfunctionfilter_kernel(tc, x_bytes, x_scale, p, om, nu, b,
                 grouped[:].rearrange("p (c i t) -> p c t i", i=4, t=4), src[:].rearrange("p t (c i) -> p c t i", i=4)
             )
 
+        def interleave_g(grouped, src):
+            for k in range(4):
+                nc.gpsimd.tensor_scalar(
+                    grouped[:, 512 * k : 512 * (k + 1)].rearrange("p (d t) -> p d t", t=4),
+                    src[:].rearrange("p t d -> p d t")[:, P * k : P * (k + 1), :],
+                    1.0,
+                    0.0,
+                    op0=ALU.mult,
+                    op1=ALU.add,
+                )
+
         def p_turn(g, h):
             bank = ps_u.tile([P, 2, 2, P], F32, name="u")
             for k in range(2):
-                words = p_in[g][:, 2 * h + k, :].bitcast(F32)
+                words = p_in[h][:, k, 512 * g : 512 * (g + 1)].bitcast(F32)
                 for u in range(2):
                     nc.tensor.transpose(bank[:, k, u, :], words[:, u::2], ident[:])
             return bank
 
-        def q_turn(r, h):
+        def q_turn(r, h, warm_first=False):
             bank = ps_w.tile([P, 2, 2, P], F32, name="w")
+            if warm_first:
+                keep_warm(bank)
             for k in range(2):
                 words = q_in[r][:, 2 * h + k, :].bitcast(F32)
                 for u in range(2):
@@ -200,47 +215,55 @@ def tile_cauchytransferfunctionfilter_kernel(tc, x_bytes, x_scale, p, om, nu, b,
                     mxmm(bank[:, t, :], p_q[g], P * t, x_q[i][g], P * dc, P, g == 0, g == G - 1)
             return bank
 
-        def f_mul(i, dc, bank):
+        def f_mul(n, dc, bank):
+            i, d0, w = units[n]
+            a = 4 * (P * dc - d0)
             nc.vector.tensor_tensor(
-                f_grp[i][:, :, 512 * dc : 512 * (dc + 1)].rearrange("p r (d t) -> p r d t", t=4),
+                f_grp[n][:].rearrange("p (r f) -> p r f", r=C)[:, :, a : a + 512].rearrange("p r (d t) -> p r d t", t=4),
                 bank[:].rearrange("p t d -> p d t").unsqueeze(1).to_broadcast([P, C, P, 4]),
                 k_sb[:, dc, :, :].rearrange("p r (d t) -> p r d t", t=4),
                 op=ALU.mult,
             )
 
-        def f_quant(i, h):
-            for r in range(C):
-                nc.vector.quantize_mx(
-                    out=f_codes[i][r][:, 256 * h : 256 * (h + 1)].bitcast(FP8X4),
-                    scales=f_scales[i][r][:, 256 * h : 256 * (h + 1)],
-                    in_=f_grp[i][:, r, 1024 * h : 1024 * (h + 1)],
-                )
+        def f_quant(n):
+            nc.vector.quantize_mx(out=f_codes[n][:].bitcast(FP8X4), scales=f_scales[n][:], in_=f_grp[n][:])
 
-        def o_mm(i, h, s2, warm_first=False):
-            bank = ps_w.tile([P, 2, 256], F32, name="w")
+        def o_mm(n, s0, warm_first=False):
+            i, d0, w = units[n]
+            bank = ps_w.tile([P, 512 // w, w], F32, name="w")
             if warm_first:
                 keep_warm(bank)
-            for k in range(2):
+            for k in range(512 // w):
                 for r in range(C):
-                    mxmm(bank[:, k, :], q_q[r], P * (2 * s2 + k), (f_codes[i][r], f_scales[i][r]), 256 * h, 256, r == 0, r == C - 1)
+                    mxmm(bank[:, k, :], q_q[r], P * (s0 + k), (f_codes[n], f_scales[n]), w * r, w, r == 0, r == C - 1)
             return bank
 
-        def out_pair(i, h, s2, on_vector=False, warm_first=False):
-            bank = o_mm(i, h, s2, warm_first)
-            o_sb = outp.tile([P, 2, 256], F32, name="o_sb")
+        def o_view(i):
+            return out[i].rearrange("(j k) d -> j k d", k=SB)
+
+        def out_first(h, s2, warm_first=False):
+            bank = o_mm(h, 2 * s2, warm_first)
+            nc.scalar.copy(o_all[s2][:, :, 256 * h : 256 * (h + 1)], bank[:])
+            if h == 1:
+                nc.sync.dma_start(out=o_view(0)[:, 2 * s2 : 2 * s2 + 2, :], in_=o_all[s2][:])
+
+        def out_second(n, s0, on_vector=False):
+            i, d0, w = units[n]
+            rows = 512 // w
+            bank = o_mm(n, s0)
+            o_sb = outp.tile([P, rows, w], F32, name="o_sb")
             if on_vector:
                 nc.vector.tensor_copy(o_sb[:], bank[:])
             else:
                 nc.scalar.copy(o_sb[:], bank[:])
-            nc.sync.dma_start(
-                out=out[i].rearrange("(j k) d -> j k d", k=SB)[:, 2 * s2 : 2 * s2 + 2, 256 * h : 256 * (h + 1)], in_=o_sb[:]
-            )
+            nc.sync.dma_start(out=o_view(1)[:, s0 : s0 + rows, d0 : d0 + w], in_=o_sb[:])
 
         kb = {}
         ub = {}
         tq = {}
-        for t in range(4):
+        for t in range(3):
             widen_v(0, 0, t)
+        widen_s(0, 0, 3)
         g_square(0)
         g_square(1)
         g_square(2)
@@ -249,18 +272,18 @@ def tile_cauchytransferfunctionfilter_kernel(tc, x_bytes, x_scale, p, om, nu, b,
         g_recip(0)
         g_rsqrt(2)
         g_recip(2)
+        widen_v(0, 1, 0)
         interleave(x_q[0][0][2], x_wide[0][0])
         interleave(c_q[2], c_in)
-        widen_v(0, 1, 0)
-        quant(x_q[0][0], 0, D)
         widen_v(0, 1, 1)
+        quant(x_q[0][0], 0, D)
+        widen_v(0, 1, 2)
         quant(c_q, 0, D)
         nc.vector.tensor_scalar(b2[:], b4[:], 2.0, None, op0=ALU.mult)
         tp = [p_turn(0, 0), p_turn(0, 1)]
         for r in range(C):
             for h in range(2):
                 tq[r, h] = q_turn(r, h)
-        widen_s(0, 1, 2)
         widen_s(0, 1, 3)
         for h in range(2):
             turn_copy(p_q[0][2], h, tp[h])
@@ -270,6 +293,7 @@ def tile_cauchytransferfunctionfilter_kernel(tc, x_bytes, x_scale, p, om, nu, b,
         g_round(0, 2)
         g_real(2)
         g_imag(2)
+        quant(p_q[0], 0, M)
         g_imag(3)
         g_round(2, 2)
         tp = [p_turn(1, 0), p_turn(1, 1)]
@@ -282,21 +306,20 @@ def tile_cauchytransferfunctionfilter_kernel(tc, x_bytes, x_scale, p, om, nu, b,
         for h in range(2):
             turn_copy(p_q[1][2], h, tp[h])
         widen_s(1, 0, 2)
-        quant(p_q[0], 0, M)
         quant(gr_q, 0, M)
         quant(gi_q, 0, M)
         interleave(x_q[0][1][2], x_wide[0][1])
         quant(q_q[0], 0, 512)
+        quant(p_q[1], 0, M)
         quant(x_q[0][1], 0, D)
         quant(q_q[1], 0, 512)
-        quant(p_q[1], 0, M)
         for dc in range(2):
             for r in range(C):
                 kb[dc, r] = k_mm(dc, r)
         k_copy(0, 0, kb[0, 0])
         widen_s(1, 0, 3)
+        interleave_g(x_q[1][0][2], x_wide[1][0])
         k_copy(0, 1, kb[0, 1])
-        interleave(x_q[1][0][2], x_wide[1][0])
         ub[0] = u_mm(0, 0, True)
         kb[2, 0] = k_mm(2, 0)
         kb[2, 1] = k_mm(2, 1)
@@ -316,42 +339,44 @@ def tile_cauchytransferfunctionfilter_kernel(tc, x_bytes, x_scale, p, om, nu, b,
         ub[2] = u_mm(0, 2)
         f_mul(0, 1, ub[1])
         ub[3] = u_mm(0, 3)
-        f_mul(0, 2, ub[2])
-        f_quant(0, 0)
-        f_mul(0, 3, ub[3])
-        f_quant(0, 1)
-        for r in range(C):
-            tq[r, 2] = q_turn(r, 2)
+        f_mul(1, 2, ub[2])
+        f_quant(0)
+        f_mul(1, 3, ub[3])
+        quant(x_q[1][0], 0, D)
+        f_quant(1)
+        tq[0, 2] = q_turn(0, 2, True)
+        tq[1, 2] = q_turn(1, 2)
         for r in range(C):
             turn_copy(q_q[r][2], 2, tq[r, 2])
-        out_pair(0, 0, 0, False, True)
+        out_first(0, 0, True)
         for r in range(C):
             tq[r, 3] = q_turn(r, 3)
         turn_copy(q_q[0][2], 3, tq[0, 3])
-        out_pair(0, 0, 1)
+        out_first(0, 1)
         turn_copy(q_q[1][2], 3, tq[1, 3])
-        out_pair(0, 1, 0)
-        out_pair(0, 1, 1)
+        out_first(1, 0)
+        out_first(1, 1)
         interleave(x_q[1][1][2], x_wide[1][1])
-        quant(x_q[1][0], 0, D)
-        quant(x_q[1][1], 0, D)
         quant(q_q[0], 512, 1024)
+        quant(x_q[1][1], 0, D)
         quant(q_q[1], 512, 1024)
         ub[0] = u_mm(1, 0)
         ub[1] = u_mm(1, 1)
-        f_mul(1, 0, ub[0])
-        f_mul(1, 1, ub[1])
-        out_pair(0, 0, 2)
-        out_pair(0, 0, 3)
+        f_mul(2, 0, ub[0])
+        f_mul(2, 1, ub[1])
+        out_first(0, 2)
+        out_first(0, 3)
         ub[2] = u_mm(1, 2)
-        f_mul(1, 2, ub[2])
-        f_quant(1, 0)
-        out_pair(0, 1, 2)
+        f_mul(3, 2, ub[2])
+        f_quant(2)
+        out_first(1, 2)
         ub[3] = u_mm(1, 3)
-        f_mul(1, 3, ub[3])
-        f_quant(1, 1)
-        out_pair(0, 1, 3)
+        f_quant(3)
+        f_mul(4, 3, ub[3])
+        out_first(1, 3)
+        f_quant(4)
         for s2 in range(4):
-            out_pair(1, 0, s2)
-        for s2 in range(4):
-            out_pair(1, 1, s2, s2 % 2 == 1)
+            out_second(2, 2 * s2)
+        for n in (3, 4):
+            for s4 in range(2):
+                out_second(n, 4 * s4, n == 4 and s4 == 0)

from contextlib import ExitStack

import concourse.mybir as mybir
from concourse.masks import make_identity

F32 = mybir.dt.float32
BF16 = mybir.dt.bfloat16
U32 = mybir.dt.uint32
U8 = mybir.dt.uint8
FP8 = mybir.dt.float8_e4m3fn
FP8X4 = mybir.dt.float8_e4m3fn_x4
ACT = mybir.ActivationFunctionType
ALU = mybir.AluOpType

P = 128
B, S, D, M, N, C = 2, 1024, 512, 512, 512, 2
G = S // 512
DC = D // P
SB = S // P

FLOPS = 2 * C * M * N * D + 2 * B * M * S * D + 2 * B * C * S * M * D


def tile_cauchytransferfunctionfilter_kernel(tc, x_bytes, x_scale, p, om, nu, b, c, q, out):
    nc = tc.nc
    with ExitStack() as ctx:
        sb = ctx.enter_context(tc.tile_pool(name="sb", bufs=1))
        outp = ctx.enter_context(tc.tile_pool(name="outp", bufs=8))
        ps_u = ctx.enter_context(tc.psum_pool(name="ps_u", bufs=2))
        ps_w = ctx.enter_context(tc.psum_pool(name="ps_w", bufs=6))
        ctx.enter_context(tc.manual_schedule())

        om_row = sb.tile([P, M], BF16, name="om_row")
        nu_row = sb.tile([P, N], BF16, name="nu_row")
        ident = sb.tile([P, P], F32, name="ident")
        b4 = sb.tile([P, 4], BF16, name="b4")
        b2 = sb.tile([P, 4], F32, name="b2")
        xs = sb.tile([P, G, 4], F32, name="xs")
        warm = sb.tile([P, D], BF16, name="warm")
        scr = sb.tile([P, 2], F32, name="scr")
        x_in = [sb.tile([P, G, 4, D], U8, name=f"x_in{i}") for i in range(B)]
        c_in = sb.tile([P, 4, D], BF16, name="c_in")
        p_in = [sb.tile([P, 2, S], BF16, name=f"p_in{h}") for h in range(2)]
        q_in = [sb.tile([P, SB, M], BF16, name=f"q_in{r}") for r in range(C)]
        x_wide = [[sb.tile([P, 4, D], BF16, name=f"x_wide{i}{g}") for g in range(G)] for i in range(B)]

        def mx(width, name):
            codes = sb.tile([P, width], U32, name=name + "_codes", align_bytes=64)
            scales = sb.tile([P, width], U8, name=name + "_scales", align_bytes=64)
            grouped = sb.tile([P, width * 4], BF16, name=name + "_grp", align_bytes=64)
            return codes, scales, grouped

        gr_q = mx(M, "gr")
        gi_q = mx(M, "gi")
        c_q = mx(D, "c")
        p_q = [mx(M, f"p{g}") for g in range(G)]
        x_q = [[mx(D, f"x{i}{g}") for g in range(G)] for i in range(B)]
        q_q = [mx(S, f"q{r}") for r in range(C)]
        units = [(0, 0, 256), (0, 256, 256), (1, 0, 256), (1, 256, 128), (1, 384, 128)]
        f_codes = [sb.tile([P, C * w], U32, name=f"f_codes{n}", align_bytes=64) for n, (i, d0, w) in enumerate(units)]
        f_scales = [sb.tile([P, C * w], U8, name=f"f_scales{n}", align_bytes=64) for n, (i, d0, w) in enumerate(units)]
        f_grp = [sb.tile([P, C * w * 4], BF16, name=f"f_grp{n}", align_bytes=64) for n, (i, d0, w) in enumerate(units)]
        o_all = [sb.tile([P, 2, D], F32, name=f"o_all{n}") for n in range(SB // 2)]
        sq = sb.tile([P, M * 4], F32, name="sq")
        rt = sb.tile([P, M * 4], F32, name="rt")
        rr = sq
        g32 = sb.tile([P, M * 4], F32, name="g32")
        k_sb = sb.tile([P, DC, C, P * 4], F32, name="k_sb")

        def quant(t, a, z):
            codes, scales, grouped = t
            nc.vector.quantize_mx(out=codes[:, a:z].bitcast(FP8X4), scales=scales[:, a:z], in_=grouped[:, 4 * a : 4 * z])

        def mxmm(acc, lhs, m0, rhs, n0, n, start, stop):
            nc.tensor.matmul_mx(
                out=acc,
                lhsT=lhs[0][:, m0 : m0 + P].bitcast(FP8X4),
                lhsT_scale=lhs[1][:, m0 : m0 + P],
                rhs=rhs[0][:, n0 : n0 + n].bitcast(FP8X4),
                rhs_scale=rhs[1][:, n0 : n0 + n],
                start=start,
                stop=stop,
            )

        nc.sync.dma_start(out=om_row[127:128, :], in_=om.rearrange("(o m) -> o m", o=1))
        nc.sync.dma_start(out=nu_row[63:64, :], in_=nu.rearrange("(o m) -> o m", o=1))
        nc.vector.memset(warm[:], 0.0)
        nc.vector.memset(scr[:], 1.0)
        nc.gpsimd.memset(om_row[0:32, :], 0.0)
        nc.vector.memset(om_row[32:64, :], -1.0)
        nc.gpsimd.memset(om_row[64:127, :], 0.0)
        nc.gpsimd.memset(nu_row[0:32, :], 0.0)
        nc.gpsimd.memset(nu_row[32:63, :], 0.0)
        nc.vector.memset(nu_row[64:128, :], 1.0)
        make_identity(nc, ident[:])
        nc.scalar.dma_start(out=xs[:], in_=x_scale.rearrange("o (g p t) q -> p g (o t q)", p=P, t=4))
        nc.scalar.dma_start(out=b4[:], in_=b.rearrange("(p t) -> p t", t=4))
        for g in range(G):
            nc.sync.dma_start(out=x_in[0][:, g], in_=x_bytes[0].rearrange("(g p t) d -> p g t d", p=P, t=4)[:, g])
        nc.sync.dma_start(out=c_in[:], in_=c.rearrange("(p t) d -> p t d", t=4))
        for h in range(2):
            nc.sync.dma_start(out=p_in[h][:], in_=p.rearrange("(r t) s -> r t s", t=4)[:, 2 * h : 2 * h + 2, :])
        q_load = lambda r, h: nc.sync.dma_start(
            out=q_in[r][:, 4 * h : 4 * h + 4, :],
            in_=q[r].rearrange("(j k) m -> j k m", k=SB)[:, 4 * h : 4 * h + 4, :],
        )
        q_load(0, 0)
        q_load(1, 0)
        nc.sync.dma_start(out=x_in[1][:], in_=x_bytes[1].rearrange("(g p t) d -> p g t d", p=P, t=4))
        q_load(0, 1)
        q_load(1, 1)
        nc.scalar.activation(scr[:, 1:2], scr[:, 0:1], ACT.Abs_reciprocal_sqrt)
        e_ps = [ps_w.tile([P, P, 4], F32, name="w") for t in range(4)]
        def keep_warm(bank):
            flat = bank[:].rearrange("p a b -> p (a b)") if len(bank.shape) == 3 else bank[:].rearrange("p a b c -> p (a b c)")
            nc.tensor.matmul(flat, warm[:, 0:P], warm[:], start=True, stop=True)

        for k in range(4):
            keep_warm(e_ps[0])
        for k in range(4):
            for t in range(4):
                nc.tensor.matmul(e_ps[k][:, :, t], nu_row[:, t::4], om_row[:, k::4], start=True, stop=True)

        def chunk(tile, t, n=1):
            return tile[:, 512 * t : 512 * (t + n)]

        def g_square(t):
            nc.scalar.activation(chunk(sq, t), e_ps[t][:].rearrange("p m t -> p (m t)"), ACT.Square, scale=2.0)

        def g_rsqrt(t):
            nc.scalar.activation(chunk(rt, t, 2), chunk(sq, t, 2), ACT.Abs_reciprocal_sqrt, bias=1.0)

        def g_recip(t):
            nc.scalar.activation(chunk(rr, t, 2), chunk(rt, t, 2), ACT.Square)

        def g_real(t):
            nc.vector.tensor_tensor(
                chunk(g32, t, 2).rearrange("p (m t) -> p m t", t=4),
                chunk(rr, t, 2).rearrange("p (m t) -> p m t", t=4),
                b2[:].unsqueeze(1).to_broadcast([P, 2 * P, 4]),
                op=ALU.mult,
            )

        def g_imag(t):
            nc.vector.scalar_tensor_tensor(
                chunk(gi_q[2], t), e_ps[t][:].rearrange("p m t -> p (m t)"), 2.0, chunk(g32, t), op0=ALU.mult, op1=ALU.mult
            )

        def g_round(t, n):
            nc.gpsimd.tensor_scalar(chunk(gr_q[2], t, n), chunk(g32, t, n), 1.0, 0.0, op0=ALU.mult, op1=ALU.add)

        def widen_v(i, g, t):
            nc.vector.tensor_scalar(x_wide[i][g][:, t, :], x_in[i][:, g, t, :].bitcast(FP8), xs[:, g, t : t + 1], None, op0=ALU.mult)

        def widen_s(i, g, t):
            nc.scalar.activation(x_wide[i][g][:, t, :], x_in[i][:, g, t, :].bitcast(FP8), ACT.Copy, scale=xs[:, g, t : t + 1])

        def interleave(grouped, src):
            nc.vector.tensor_copy(
                grouped[:].rearrange("p (c i t) -> p c t i", i=4, t=4), src[:].rearrange("p t (c i) -> p c t i", i=4)
            )

        def interleave_g(grouped, src):
            for k in range(4):
                nc.gpsimd.tensor_scalar(
                    grouped[:, 512 * k : 512 * (k + 1)].rearrange("p (d t) -> p d t", t=4),
                    src[:].rearrange("p t d -> p d t")[:, P * k : P * (k + 1), :],
                    1.0,
                    0.0,
                    op0=ALU.mult,
                    op1=ALU.add,
                )

        def p_turn(g, h):
            bank = ps_u.tile([P, 2, 2, P], F32, name="u")
            for k in range(2):
                words = p_in[h][:, k, 512 * g : 512 * (g + 1)].bitcast(F32)
                for u in range(2):
                    nc.tensor.transpose(bank[:, k, u, :], words[:, u::2], ident[:])
            return bank

        def q_turn(r, h, warm_first=False):
            bank = ps_w.tile([P, 2, 2, P], F32, name="w")
            if warm_first:
                keep_warm(bank)
            for k in range(2):
                words = q_in[r][:, 2 * h + k, :].bitcast(F32)
                for u in range(2):
                    nc.tensor.transpose(bank[:, k, u, :], words[:, u::2], ident[:])
            return bank

        def turn_copy(grouped, h, bank):
            dst = grouped[:, 1024 * h : 1024 * (h + 1)].bitcast(F32).rearrange("p (k r u) -> p k r u", k=2, u=2)
            nc.scalar.copy(dst, bank[:].rearrange("p k u r -> p k r u"))

        def k_mm(dc, r, warm_first=False):
            bank = ps_w.tile([P, 4, P], F32, name="w")
            if warm_first:
                keep_warm(bank)
            for t in range(4):
                mxmm(bank[:, t, :], (gr_q, gi_q)[r], P * t, c_q, P * dc, P, True, True)
            return bank

        def k_copy(dc, r, bank):
            nc.scalar.copy(
                k_sb[:, dc, r, :].rearrange("p (d t) -> p d t", t=4), bank[:].rearrange("p t d -> p d t")
            )

        def u_mm(i, dc, warm_first=False):
            bank = ps_u.tile([P, 4, P], F32, name="u")
            if warm_first:
                keep_warm(bank)
            for t in range(4):
                for g in range(G):
                    mxmm(bank[:, t, :], p_q[g], P * t, x_q[i][g], P * dc, P, g == 0, g == G - 1)
            return bank

        def f_mul(n, dc, bank):
            i, d0, w = units[n]
            a = 4 * (P * dc - d0)
            nc.vector.tensor_tensor(
                f_grp[n][:].rearrange("p (r f) -> p r f", r=C)[:, :, a : a + 512].rearrange("p r (d t) -> p r d t", t=4),
                bank[:].rearrange("p t d -> p d t").unsqueeze(1).to_broadcast([P, C, P, 4]),
                k_sb[:, dc, :, :].rearrange("p r (d t) -> p r d t", t=4),
                op=ALU.mult,
            )

        def f_quant(n):
            nc.vector.quantize_mx(out=f_codes[n][:].bitcast(FP8X4), scales=f_scales[n][:], in_=f_grp[n][:])

        def o_mm(n, s0, warm_first=False):
            i, d0, w = units[n]
            bank = ps_w.tile([P, 512 // w, w], F32, name="w")
            if warm_first:
                keep_warm(bank)
            for k in range(512 // w):
                for r in range(C):
                    mxmm(bank[:, k, :], q_q[r], P * (s0 + k), (f_codes[n], f_scales[n]), w * r, w, r == 0, r == C - 1)
            return bank

        def o_view(i):
            return out[i].rearrange("(j k) d -> j k d", k=SB)

        def out_first(h, s2, warm_first=False):
            bank = o_mm(h, 2 * s2, warm_first)
            nc.scalar.copy(o_all[s2][:, :, 256 * h : 256 * (h + 1)], bank[:])
            if h == 1:
                nc.sync.dma_start(out=o_view(0)[:, 2 * s2 : 2 * s2 + 2, :], in_=o_all[s2][:])

        def out_second(n, s0, on_vector=False):
            i, d0, w = units[n]
            rows = 512 // w
            bank = o_mm(n, s0)
            o_sb = outp.tile([P, rows, w], F32, name="o_sb")
            if on_vector:
                nc.vector.tensor_copy(o_sb[:], bank[:])
            else:
                nc.scalar.copy(o_sb[:], bank[:])
            nc.sync.dma_start(out=o_view(1)[:, s0 : s0 + rows, d0 : d0 + w], in_=o_sb[:])

        kb = {}
        ub = {}
        tq = {}
        for t in range(3):
            widen_v(0, 0, t)
        widen_s(0, 0, 3)
        g_square(0)
        g_square(1)
        g_square(2)
        g_rsqrt(0)
        g_square(3)
        g_recip(0)
        g_rsqrt(2)
        g_recip(2)
        widen_v(0, 1, 0)
        interleave(x_q[0][0][2], x_wide[0][0])
        interleave(c_q[2], c_in)
        widen_v(0, 1, 1)
        quant(x_q[0][0], 0, D)
        widen_v(0, 1, 2)
        quant(c_q, 0, D)
        nc.vector.tensor_scalar(b2[:], b4[:], 2.0, None, op0=ALU.mult)
        tp = [p_turn(0, 0), p_turn(0, 1)]
        for r in range(C):
            for h in range(2):
                tq[r, h] = q_turn(r, h)
        widen_s(0, 1, 3)
        for h in range(2):
            turn_copy(p_q[0][2], h, tp[h])
        g_real(0)
        g_imag(0)
        g_imag(1)
        g_round(0, 2)
        g_real(2)
        g_imag(2)
        quant(p_q[0], 0, M)
        g_imag(3)
        g_round(2, 2)
        tp = [p_turn(1, 0), p_turn(1, 1)]
        widen_s(1, 0, 0)
        turn_copy(q_q[0][2], 0, tq[0, 0])
        turn_copy(q_q[0][2], 1, tq[0, 1])
        widen_s(1, 0, 1)
        turn_copy(q_q[1][2], 0, tq[1, 0])
        turn_copy(q_q[1][2], 1, tq[1, 1])
        for h in range(2):
            turn_copy(p_q[1][2], h, tp[h])
        widen_s(1, 0, 2)
        quant(gr_q, 0, M)
        quant(gi_q, 0, M)
        interleave(x_q[0][1][2], x_wide[0][1])
        quant(q_q[0], 0, 512)
        quant(p_q[1], 0, M)
        quant(x_q[0][1], 0, D)
        quant(q_q[1], 0, 512)
        for dc in range(2):
            for r in range(C):
                kb[dc, r] = k_mm(dc, r)
        k_copy(0, 0, kb[0, 0])
        widen_s(1, 0, 3)
        interleave_g(x_q[1][0][2], x_wide[1][0])
        k_copy(0, 1, kb[0, 1])
        ub[0] = u_mm(0, 0, True)
        kb[2, 0] = k_mm(2, 0)
        kb[2, 1] = k_mm(2, 1)
        ub[1] = u_mm(0, 1)
        kb[3, 0] = k_mm(3, 0)
        kb[3, 1] = k_mm(3, 1)
        k_copy(1, 0, kb[1, 0])
        k_copy(1, 1, kb[1, 1])
        k_copy(2, 0, kb[2, 0])
        k_copy(2, 1, kb[2, 1])
        widen_s(1, 1, 0)
        k_copy(3, 0, kb[3, 0])
        k_copy(3, 1, kb[3, 1])
        for t in range(1, 4):
            widen_s(1, 1, t)
        f_mul(0, 0, ub[0])
        ub[2] = u_mm(0, 2)
        f_mul(0, 1, ub[1])
        ub[3] = u_mm(0, 3)
        f_mul(1, 2, ub[2])
        f_quant(0)
        f_mul(1, 3, ub[3])
        quant(x_q[1][0], 0, D)
        f_quant(1)
        tq[0, 2] = q_turn(0, 2, True)
        tq[1, 2] = q_turn(1, 2)
        for r in range(C):
            turn_copy(q_q[r][2], 2, tq[r, 2])
        out_first(0, 0, True)
        for r in range(C):
            tq[r, 3] = q_turn(r, 3)
        turn_copy(q_q[0][2], 3, tq[0, 3])
        out_first(0, 1)
        turn_copy(q_q[1][2], 3, tq[1, 3])
        out_first(1, 0)
        out_first(1, 1)
        interleave(x_q[1][1][2], x_wide[1][1])
        quant(q_q[0], 512, 1024)
        quant(x_q[1][1], 0, D)
        quant(q_q[1], 512, 1024)
        ub[0] = u_mm(1, 0)
        ub[1] = u_mm(1, 1)
        f_mul(2, 0, ub[0])
        f_mul(2, 1, ub[1])
        out_first(0, 2)
        out_first(0, 3)
        ub[2] = u_mm(1, 2)
        f_mul(3, 2, ub[2])
        f_quant(2)
        out_first(1, 2)
        ub[3] = u_mm(1, 3)
        f_quant(3)
        f_mul(4, 3, ub[3])
        out_first(1, 3)
        f_quant(4)
        for s2 in range(4):
            out_second(2, 2 * s2)
        for n in (3, 4):
            for s4 in range(2):
                out_second(n, 4 * s4, n == 4 and s4 == 0)
